import numpy as np
import ml_dtypes


def mxq(x, axis, fmt="e4m3"):
    dtype, down = {"e4m3": (ml_dtypes.float8_e4m3fn, 7), "e5m2": (ml_dtypes.float8_e5m2, 14)}[fmt]
    v = np.moveaxis(np.asarray(x, np.float32).astype(ml_dtypes.bfloat16).astype(np.float64), axis, -1)
    blocks = v.reshape(v.shape[:-1] + (-1, 32))
    amax = np.abs(blocks).max(-1, keepdims=True)
    byte = np.maximum(np.where(amax > 0, np.frexp(amax)[1] - 1 + 127, 0) - down, 1)
    scale = np.exp2(byte - 127.0)
    codes = (blocks / scale).astype(np.float32).astype(dtype).astype(np.float64)
    return np.moveaxis((codes * scale).reshape(v.shape), -1, axis)


WIDE = False


def mx_kscale(k):
    if not WIDE:
        return np.ones(k)
    levels = np.array([10, -10, 5, -5, 0])
    if k % 512:
        return np.exp2(np.random.permutation(np.resize(levels, k // 32))).repeat(32)
    a = np.empty((k // 512, 16))
    for p in range(k // 512):
        a[p, :8] = np.random.permutation(np.resize(levels, 8))
        for g in range(8):
            far = levels[np.abs(levels - a[p, g]) >= 10]
            a[p, g + 8] = far[np.random.randint(len(far))]
    return np.exp2(a.ravel()).repeat(32)


def f64(x):
    return np.asarray(x).astype(np.float64)


def striped(idx):
    return np.tile(np.asarray(idx).reshape(-1, 16).T, (8, 1)).astype(np.uint16)


def unstriped(offs):
    return offs[:16].T.reshape(-1).astype(np.int64)


E2M1 = np.array([0.0, 0.5, 1.0, 1.5, 2.0, 3.0, 4.0, 6.0, -0.0, -0.5, -1.0, -1.5, -2.0, -3.0, -4.0, -6.0])


def pack_weight(w, fmt):
    k, n = w.shape
    w = f64(np.asarray(w, np.float32).astype(ml_dtypes.bfloat16)).reshape(k // 32, 32, n)
    amax = np.abs(w).max(1)
    if fmt == "e4m3":
        byte = np.frexp(amax)[1] - 1 + 127 - 7
    else:
        mant, ex = np.frexp(amax / 6.0)
        byte = np.where(mant > 0.5, ex, ex - 1) + 127
    byte = np.clip(np.where(amax > 0, byte, 1), 1, 254)
    scaled = (w * np.exp2(127.0 - byte)[:, None, :]).reshape(k, n).astype(np.float32)
    by_word = np.ascontiguousarray(scaled.reshape(k // 512, 128, 4, n).transpose(0, 1, 3, 2))
    if fmt == "e4m3":
        words = by_word.astype(ml_dtypes.float8_e4m3fn).view(np.uint8)
    else:
        c = by_word.astype(ml_dtypes.float4_e2m1fn).view(np.uint8) & 0xF
        words = (c[..., 0::2] | (c[..., 1::2] << 4)).reshape(k // 512, 128, 2 * n)
    return np.ascontiguousarray(words), np.ascontiguousarray(byte.astype(np.uint8).reshape(k // 512, 16, n))


def unpack_weight(words, scales, fmt):
    g, _, n = scales.shape
    words = np.ascontiguousarray(words).reshape(g, 128, n, -1)
    if fmt == "e4m3":
        vals = words.view(ml_dtypes.float8_e4m3fn).astype(np.float64)
    else:
        nib = np.empty((g, 128, n, 4), np.uint8)
        nib[..., 0::2] = words & 0xF
        nib[..., 1::2] = words >> 4
        vals = E2M1[nib]
    vals = vals * np.repeat(np.exp2(scales.astype(np.float64) - 127.0), 8, axis=1)[..., None]
    return vals.transpose(0, 1, 3, 2).reshape(g * 512, n)


D, T, I, J, U, X, Z, E, N = 512, 2048, 512, 512, 1024, 1024, 1024, 512, 64


def setup_inputs():
    n = np.random.standard_normal
    idx = np.random.permutation(T)[:I]
    idx2 = np.random.permutation(U)[:J]
    idx3 = np.random.permutation(X)[:I]
    idx4 = np.random.permutation(Z)[:J]
    fd = mx_kscale(D)
    fi = mx_kscale(I)
    ti = np.ones(T)
    ti[idx] = fi
    keysp = pack_weight(n((D, T)) / fd[:, None], "e4m3")
    morep = pack_weight(n((D, X)) / fd[:, None], "e4m3")
    return {
        "keys_words": keysp[0],
        "keys_scales": keysp[1],
        "notes": (n((D, U)) * 1.0 / np.sqrt(D) * fd[:, None]).astype(np.float32),
        "more_words": morep[0],
        "more_scales": morep[1],
        "users2": (n((D, Z)) * 1.0 / np.sqrt(D) * fd[:, None]).astype(np.float32),
        "rowf": (np.random.uniform(0.02, 0.08, (I, 1)) * fi[:, None]).astype(np.float32),
        "vals": (n((E, T)) / ti).astype(np.float32),
        "offs": striped(idx),
        "offs2": striped(idx2),
        "offs3": striped(idx3),
        "offs4": striped(idx4),
    }


def reference(keys_words, keys_scales, notes, more_words, more_scales, users2, rowf, vals, offs, offs2, offs3, offs4):
    idx = unstriped(offs)
    idx2 = unstriped(offs2)
    idx3 = unstriped(offs3)
    idx4 = unstriped(offs4)
    keysu = unpack_weight(keys_words, keys_scales, "e4m3")
    moreu = unpack_weight(more_words, more_scales, "e4m3")
    keysidxg = keysu[:, idx]
    notesidx2q = mxq(f64(notes)[:, idx2], 0, "e4m3")
    moreidx3g = moreu[:, idx3]
    users2idx4q = mxq(f64(users2)[:, idx4], 0, "e4m3")
    g0 = keysidxg.T @ notesidx2q + moreidx3g.T @ users2idx4q
    gr1 = g0 * f64(rowf)
    vt1 = f64(vals)[:, idx].T
    vt1q = mxq(vt1, 0, "e4m3")
    gr1q = mxq(gr1, 0, "e4m3")
    o = vt1q.T @ gr1q
    y = o.reshape(E, N, J // N).max(axis=2)
    return y

@@ -1,0 +1,213 @@
+from contextlib import ExitStack
+
+import concourse.mybir as mybir
+from concourse.masks import make_identity
+
+D, T, I, J, U, X, Z, E, N = 512, 2048, 512, 512, 1024, 1024, 1024, 512, 64
+FLOPS = 2 * (2 * D * I * J + I * E * J)
+
+F32 = mybir.dt.float32
+BF16 = mybir.dt.bfloat16
+I32 = mybir.dt.int32
+U32 = mybir.dt.uint32
+U16 = mybir.dt.uint16
+U8 = mybir.dt.uint8
+FP8X4 = mybir.dt.float8_e4m3fn_x4
+COPY = mybir.ActivationFunctionType.Copy
+
+P = 128
+PACK = 4
+RUN = J // N
+MORE_ROW = 4
+
+
+def tile_attend_tab_twosum_bestruns_kernel(
+    tc, keys_words, keys_scales, notes, more_words, more_scales, users2, rowf, vals, offs, offs2, offs3, offs4, out
+):
+    nc = tc.nc
+    with ExitStack() as ctx:
+        lists = ctx.enter_context(tc.tile_pool(name="lists", bufs=1))
+        held = ctx.enter_context(tc.tile_pool(name="held", bufs=1))
+        psum_g = ctx.enter_context(tc.psum_pool(name="psum_g", bufs=1))
+        psum_t = ctx.enter_context(tc.psum_pool(name="psum_t", bufs=2))
+        psum_o = ctx.enter_context(tc.psum_pool(name="psum_o", bufs=2))
+
+        l_key = lists.tile([P, I // 16], U16, name="l_key")
+        l_note = lists.tile([P, J // 16], U16, name="l_note")
+        l_more = lists.tile([P, I // 16], U16, name="l_more")
+        l_user = lists.tile([P, J // 16], U16, name="l_user")
+
+        kw = held.tile([P, T], U32, name="kw", align_bytes=64)
+        ks = held.tile([P, T], U8, name="ks", align_bytes=64)
+        mw = held.tile([P, X], U32, name="mw", align_bytes=64)
+        ms = held.tile([P, X], U8, name="ms", align_bytes=64)
+        note_planes = [held.tile([P, U], F32, name=f"note{t}", align_bytes=64) for t in range(PACK)]
+        user_planes = [held.tile([P, Z], F32, name=f"user{t}", align_bytes=64) for t in range(PACK)]
+        val_tiles = [held.tile([P, T], F32, name=f"val{k}", align_bytes=64) for k in range(E // P)]
+        rf = held.tile([P, PACK], F32, name="rf", align_bytes=64)
+        ident = held.tile([P, P], F32, name="ident", align_bytes=64)
+
+        nc.vector.memset(ks[:].bitcast(I32), 0)
+        nc.vector.memset(ms[:].bitcast(I32), 0)
+        make_identity(nc, ident[:])
+
+        def load_scale_rows(dst, src, r, row0):
+            nc.sync.dma_start(out=dst[row0 + r : P : 32, :].bitcast(I32), in_=src[0, r:16:4, :].bitcast(I32))
+
+        notes_v = notes.rearrange("(p t) u -> t p u", t=PACK)
+        users_v = users2.rearrange("(p t) u -> t p u", t=PACK)
+        big = [
+            (kw[:].bitcast(I32), keys_words[0].rearrange("p n t -> p (n t)").bitcast(I32)),
+            (mw[:].bitcast(I32), more_words[0].rearrange("p n t -> p (n t)").bitcast(I32)),
+        ]
+        big = big + [(note_planes[t][:], notes_v[t]) for t in range(PACK)]
+        big = big + [(user_planes[t][:], users_v[t]) for t in range(PACK)]
+        big = big + [(val_tiles[k][:], vals[k * P : (k + 1) * P, :]) for k in range(E // P)]
+        small = {
+            0: [lambda: nc.sync.dma_start(l_key[:], offs)],
+            1: [lambda: nc.sync.dma_start(l_more[:], offs3), lambda: nc.sync.dma_start(l_note[:], offs2)],
+            2: [lambda: load_scale_rows(ks, keys_scales, 0, 0), lambda: load_scale_rows(ks, keys_scales, 1, 0)],
+            3: [lambda: load_scale_rows(ks, keys_scales, 2, 0), lambda: load_scale_rows(ks, keys_scales, 3, 0)],
+            4: [lambda: load_scale_rows(ms, more_scales, 0, MORE_ROW), lambda: load_scale_rows(ms, more_scales, 1, MORE_ROW)],
+            5: [lambda: load_scale_rows(ms, more_scales, 2, MORE_ROW), lambda: load_scale_rows(ms, more_scales, 3, MORE_ROW)],
+            6: [lambda: nc.sync.dma_start(l_user[:], offs4)],
+            7: [lambda: nc.sync.dma_start(out=rf[:], in_=rowf.rearrange("(p t) o -> p (t o)", t=PACK))],
+        }
+        for n, (dst, src) in enumerate(big):
+            nc.sync.dma_start(out=dst, in_=src)
+            for load in small.get(n, []):
+                load()
+
+        kw_g = held.tile([P, I], U32, name="kw_g", align_bytes=64)
+        ks_g = held.tile([P, I], U8, name="ks_g", align_bytes=64)
+        mw_g = held.tile([P, I], U32, name="mw_g", align_bytes=64)
+        ms_g = held.tile([P, I], U8, name="ms_g", align_bytes=64)
+
+        def dealt_gather(dst, window, offsets):
+            nc.vector.tensor_copy(dst[:].rearrange("p (r s) -> p s r", r=PACK), window[:].indirect(offsets[:]))
+
+        dealt_gather(kw_g, kw, l_key)
+        dealt_gather(mw_g, mw, l_more)
+
+        note_g = held.tile([P, PACK, J], BF16, name="note_g", align_bytes=64)
+        for t in range(PACK):
+            nc.scalar.activation(note_g[:, t, :], note_planes[t][:].indirect(l_note[:]), COPY)
+        dealt_gather(ks_g, ks, l_key)
+        dealt_gather(ms_g, ms, l_more)
+
+        def weave(engine_copy, dst, src):
+            engine_copy(
+                out=dst.rearrange("p (c i) t -> p c t i", i=4),
+                in_=src.rearrange("p t (c i) -> p c t i", i=4),
+            )
+
+        note_w = held.tile([P, J, PACK], BF16, name="note_w", align_bytes=64)
+        note_c = held.tile([P, J], U32, name="note_c", align_bytes=64)
+        note_s = held.tile([P, J], U8, name="note_s", align_bytes=64)
+        weave(nc.vector.tensor_copy, note_w[:], note_g[:])
+        nc.vector.quantize_mx(out=note_c[:].bitcast(FP8X4), scales=note_s[:], in_=note_w[:].rearrange("p j t -> p (j t)"))
+
+        nblk = J // P
+        g_banks = [psum_g.tile([P, PACK, P], F32, name=f"g{b}") for b in range(nblk)]
+        for b in range(nblk):
+            cols = slice(b * P, (b + 1) * P)
+            for r in range(PACK):
+                rows = slice(r * P, (r + 1) * P)
+                nc.tensor.matmul_mx(
+                    out=g_banks[b][:, r, :],
+                    lhsT=kw_g[:, rows].bitcast(FP8X4),
+                    lhsT_scale=ks_g[:, rows],
+                    rhs=note_c[:, cols].bitcast(FP8X4),
+                    rhs_scale=note_s[:, cols],
+                    start=(r == 0),
+                    stop=False,
+                )
+
+        half = J // 2
+        user_g = held.tile([P, PACK, J], BF16, name="user_g", align_bytes=64)
+        for t in range(PACK - 1):
+            nc.scalar.activation(user_g[:, t, :], user_planes[t][:].indirect(l_user[:]), COPY)
+        last = PACK - 1
+        nc.vector.tensor_copy(user_g[:, last, :half], user_planes[last][:].indirect(l_user[:, : half // 16]))
+        nc.scalar.activation(user_g[:, last, half:], user_planes[last][:].indirect(l_user[:, half // 16 :]), COPY)
+
+        user_w = [held.tile([P, half, PACK], BF16, name=f"user_w{h}", align_bytes=64) for h in range(2)]
+        user_c = [held.tile([P, half], U32, name=f"user_c{h}", align_bytes=64) for h in range(2)]
+        user_s = [held.tile([P, half], U8, name=f"user_s{h}", align_bytes=64) for h in range(2)]
+        weave(nc.vector.tensor_copy, user_w[0][:], user_g[:, :, :half])
+        weave(nc.scalar.copy, user_w[1][:], user_g[:, :, half:])
+        for h in range(2):
+            nc.vector.quantize_mx(
+                out=user_c[h][:].bitcast(FP8X4), scales=user_s[h][:], in_=user_w[h][:].rearrange("p j t -> p (j t)")
+            )
+        for b in range(nblk):
+            h, c0 = divmod(b * P, half)
+            cols = slice(c0, c0 + P)
+            for r in range(PACK):
+                rows = slice(r * P, (r + 1) * P)
+                nc.tensor.matmul_mx(
+                    out=g_banks[b][:, r, :],
+                    lhsT=mw_g[:, rows].bitcast(FP8X4),
+                    lhsT_scale=ms_g[MORE_ROW:, rows],
+                    rhs=user_c[h][:, cols].bitcast(FP8X4),
+                    rhs_scale=user_s[h][:, cols],
+                    start=False,
+                    stop=(r == PACK - 1),
+                )
+
+        g_w = [held.tile([P, P, PACK], BF16, name=f"g_w{b}", align_bytes=64) for b in range(nblk)]
+        g_c = held.tile([P, J], U32, name="g_c", align_bytes=64)
+        g_s = held.tile([P, J], U8, name="g_s", align_bytes=64)
+
+        def scale_rows(b):
+            nc.vector.tensor_tensor(
+                g_w[b][:],
+                g_banks[b][:].rearrange("p r j -> p j r"),
+                rf[:].unsqueeze(1).to_broadcast([P, P, PACK]),
+                mybir.AluOpType.mult,
+            )
+
+        def quantise_g(b):
+            cols = slice(b * P, (b + 1) * P)
+            nc.vector.quantize_mx(
+                out=g_c[:, cols].bitcast(FP8X4), scales=g_s[:, cols], in_=g_w[b][:].rearrange("p j t -> p (j t)")
+            )
+
+        for b in range(nblk + 1):
+            if b < nblk:
+                scale_rows(b)
+            if b > 0:
+                quantise_g(b - 1)
+
+        ntile = E // P
+        for k in range(ntile):
+            val_g = held.tile([P, I], BF16, name=f"val_g{k}", align_bytes=64)
+            if k < ntile - 1:
+                nc.scalar.activation(val_g[:], val_tiles[k][:].indirect(l_key[:]), COPY)
+            else:
+                nc.vector.tensor_copy(val_g[:, : I // 2], val_tiles[k][:].indirect(l_key[:, : I // 32]))
+                nc.scalar.activation(val_g[:, I // 2 :], val_tiles[k][:].indirect(l_key[:, I // 32 :]), COPY)
+            words = val_g[:].bitcast(F32)
+            turned = psum_t.tile([P, 2, P], F32, name="turned")
+            for u in range(2):
+                nc.tensor.transpose(turned[:, u, :], words[:, u : I // 2 : 2], ident[:])
+            val_w = held.tile([P, P, PACK], BF16, name=f"val_w{k}", align_bytes=64)
+            nc.scalar.copy(out=val_w[:].bitcast(F32), in_=turned[:].rearrange("p u e -> p e u"))
+            val_c = held.tile([P, P], U32, name=f"val_c{k}", align_bytes=64)
+            val_s = held.tile([P, P], U8, name=f"val_s{k}", align_bytes=64)
+            nc.vector.quantize_mx(out=val_c[:].bitcast(FP8X4), scales=val_s[:], in_=val_w[:].rearrange("p e t -> p (e t)"))
+            o_bank = psum_o.tile([P, J], F32, name="o_bank")
+            nc.tensor.matmul_mx(
+                out=o_bank[:],
+                lhsT=val_c[:].bitcast(FP8X4),
+                lhsT_scale=val_s[:],
+                rhs=g_c[:].bitcast(FP8X4),
+                rhs_scale=g_s[:],
+                start=True,
+                stop=True,
+            )
+            best = held.tile([P, N], F32, name=f"best{k}", align_bytes=64)
+            nc.vector.tensor_reduce(
+                best[:], o_bank[:].rearrange("p (n c) -> p n c", c=RUN), mybir.AxisListType.X, mybir.AluOpType.max
+            )
+            nc.sync.dma_start(out=out[k * P : (k + 1) * P, :], in_=best[:])

@@ -29,8 +29,7 @@ def tile_attend_tab_twosum_bestruns_kernel(
         lists = ctx.enter_context(tc.tile_pool(name="lists", bufs=1))
         held = ctx.enter_context(tc.tile_pool(name="held", bufs=1))
         psum_g = ctx.enter_context(tc.psum_pool(name="psum_g", bufs=1))
-        psum_t = ctx.enter_context(tc.psum_pool(name="psum_t", bufs=2))
-        psum_o = ctx.enter_context(tc.psum_pool(name="psum_o", bufs=2))
+        psum_v = ctx.enter_context(tc.psum_pool(name="psum_v", bufs=1))
 
         l_key = lists.tile([P, I // 16], U16, name="l_key")
         l_note = lists.tile([P, J // 16], U16, name="l_note")
@@ -41,9 +40,12 @@ def tile_attend_tab_twosum_bestruns_kernel(
         ks = held.tile([P, T], U8, name="ks", align_bytes=64)
         mw = held.tile([P, X], U32, name="mw", align_bytes=64)
         ms = held.tile([P, X], U8, name="ms", align_bytes=64)
-        note_planes = [held.tile([P, U], F32, name=f"note{t}", align_bytes=64) for t in range(PACK)]
-        user_planes = [held.tile([P, Z], F32, name=f"user{t}", align_bytes=64) for t in range(PACK)]
-        val_tiles = [held.tile([P, T], F32, name=f"val{k}", align_bytes=64) for k in range(E // P)]
+        note_pairs = [held.tile([P, 2, U], F32, name=f"note{u}", align_bytes=64) for u in range(2)]
+        user_pair = held.tile([P, 2, Z], F32, name="user_pair", align_bytes=64)
+        user_late = [held.tile([P, Z], F32, name=f"user_late{t}", align_bytes=64) for t in range(2)]
+        note_planes = [note_pairs[t // 2][:, t % 2, :] for t in range(PACK)]
+        user_planes = [user_pair[:, 0, :], user_pair[:, 1, :], user_late[0][:], user_late[1][:]]
+        val_tiles = [held.tile([P, T], F32, name=f"val{k}", tag=f"val{k}", align_bytes=64) for k in range(E // P)]
         rf = held.tile([P, PACK], F32, name="rf", align_bytes=64)
         ident = held.tile([P, P], F32, name="ident", align_bytes=64)
 
@@ -51,32 +53,29 @@ def tile_attend_tab_twosum_bestruns_kernel(
         nc.vector.memset(ms[:].bitcast(I32), 0)
         make_identity(nc, ident[:])
 
-        def load_scale_rows(dst, src, r, row0):
+        def load_scale_rows(dst, src, row0, r):
             nc.sync.dma_start(out=dst[row0 + r : P : 32, :].bitcast(I32), in_=src[0, r:16:4, :].bitcast(I32))
 
-        notes_v = notes.rearrange("(p t) u -> t p u", t=PACK)
-        users_v = users2.rearrange("(p t) u -> t p u", t=PACK)
-        big = [
-            (kw[:].bitcast(I32), keys_words[0].rearrange("p n t -> p (n t)").bitcast(I32)),
-            (mw[:].bitcast(I32), more_words[0].rearrange("p n t -> p (n t)").bitcast(I32)),
-        ]
-        big = big + [(note_planes[t][:], notes_v[t]) for t in range(PACK)]
-        big = big + [(user_planes[t][:], users_v[t]) for t in range(PACK)]
-        big = big + [(val_tiles[k][:], vals[k * P : (k + 1) * P, :]) for k in range(E // P)]
-        small = {
-            0: [lambda: nc.sync.dma_start(l_key[:], offs)],
-            1: [lambda: nc.sync.dma_start(l_more[:], offs3), lambda: nc.sync.dma_start(l_note[:], offs2)],
-            2: [lambda: load_scale_rows(ks, keys_scales, 0, 0), lambda: load_scale_rows(ks, keys_scales, 1, 0)],
-            3: [lambda: load_scale_rows(ks, keys_scales, 2, 0), lambda: load_scale_rows(ks, keys_scales, 3, 0)],
-            4: [lambda: load_scale_rows(ms, more_scales, 0, MORE_ROW), lambda: load_scale_rows(ms, more_scales, 1, MORE_ROW)],
-            5: [lambda: load_scale_rows(ms, more_scales, 2, MORE_ROW), lambda: load_scale_rows(ms, more_scales, 3, MORE_ROW)],
-            6: [lambda: nc.sync.dma_start(l_user[:], offs4)],
-            7: [lambda: nc.sync.dma_start(out=rf[:], in_=rowf.rearrange("(p t) o -> p (t o)", t=PACK))],
-        }
-        for n, (dst, src) in enumerate(big):
-            nc.sync.dma_start(out=dst, in_=src)
-            for load in small.get(n, []):
-                load()
+        notes_v = notes.rearrange("(p t) u -> p t u", t=PACK)
+        users_v = users2.rearrange("(p t) u -> p t u", t=PACK)
+        nc.sync.dma_start(out=note_pairs[0][:], in_=notes_v[:, 0:2, :])
+        nc.sync.dma_start(l_note[:], offs2)
+        nc.sync.dma_start(l_key[:], offs)
+        nc.sync.dma_start(out=kw[:].bitcast(I32), in_=keys_words[0].rearrange("p n t -> p (n t)").bitcast(I32))
+        for r in range(4):
+            load_scale_rows(ks, keys_scales, 0, r)
+        nc.sync.dma_start(out=note_pairs[1][:], in_=notes_v[:, 2:4, :])
+        nc.sync.dma_start(l_user[:], offs4)
+        nc.sync.dma_start(l_more[:], offs3)
+        nc.sync.dma_start(out=user_pair[:], in_=users_v[:, 0:2, :])
+        for r in range(4):
+            load_scale_rows(ms, more_scales, MORE_ROW, r)
+        nc.sync.dma_start(out=mw[:].bitcast(I32), in_=more_words[0].rearrange("p n t -> p (n t)").bitcast(I32))
+        nc.sync.dma_start(out=user_late[0][:], in_=users_v[:, 2, :])
+        nc.sync.dma_start(out=rf[:], in_=rowf.rearrange("(p t) o -> p (t o)", t=PACK))
+        nc.sync.dma_start(out=user_late[1][:], in_=users_v[:, 3, :])
+        for k in range(E // P):
+            nc.sync.dma_start(out=val_tiles[k][:], in_=vals[k * P : (k + 1) * P, :])
 
         kw_g = held.tile([P, I], U32, name="kw_g", align_bytes=64)
         ks_g = held.tile([P, I], U8, name="ks_g", align_bytes=64)
@@ -87,13 +86,15 @@ def tile_attend_tab_twosum_bestruns_kernel(
             nc.vector.tensor_copy(dst[:].rearrange("p (r s) -> p s r", r=PACK), window[:].indirect(offsets[:]))
 
         dealt_gather(kw_g, kw, l_key)
-        dealt_gather(mw_g, mw, l_more)
 
-        note_g = held.tile([P, PACK, J], BF16, name="note_g", align_bytes=64)
+        note_g = held.tile([P, PACK, J], F32, name="note_g", align_bytes=64)
         for t in range(PACK):
-            nc.scalar.activation(note_g[:, t, :], note_planes[t][:].indirect(l_note[:]), COPY)
-        dealt_gather(ks_g, ks, l_key)
-        dealt_gather(ms_g, ms, l_more)
+            if t == 3:
+                dealt_gather(ks_g, ks, l_key)
+            if t % 2 == 0:
+                nc.scalar.activation(note_g[:, t, :], note_planes[t].indirect(l_note[:]), COPY)
+            else:
+                nc.vector.tensor_copy(note_g[:, t, :], note_planes[t].indirect(l_note[:]))
 
         def weave(engine_copy, dst, src):
             engine_copy(
@@ -106,6 +107,9 @@ def tile_attend_tab_twosum_bestruns_kernel(
         note_s = held.tile([P, J], U8, name="note_s", align_bytes=64)
         weave(nc.vector.tensor_copy, note_w[:], note_g[:])
         nc.vector.quantize_mx(out=note_c[:].bitcast(FP8X4), scales=note_s[:], in_=note_w[:].rearrange("p j t -> p (j t)"))
+
+        dealt_gather(ms_g, ms, l_more)
+        dealt_gather(mw_g, mw, l_more)
 
         nblk = J // P
         g_banks = [psum_g.tile([P, PACK, P], F32, name=f"g{b}") for b in range(nblk)]
@@ -124,12 +128,12 @@ def tile_attend_tab_twosum_bestruns_kernel(
                 )
 
         half = J // 2
-        user_g = held.tile([P, PACK, J], BF16, name="user_g", align_bytes=64)
+        user_g = held.tile([P, PACK, J], F32, name="user_g", align_bytes=64)
         for t in range(PACK - 1):
-            nc.scalar.activation(user_g[:, t, :], user_planes[t][:].indirect(l_user[:]), COPY)
+            nc.scalar.activation(user_g[:, t, :], user_planes[t].indirect(l_user[:]), COPY)
         last = PACK - 1
-        nc.vector.tensor_copy(user_g[:, last, :half], user_planes[last][:].indirect(l_user[:, : half // 16]))
-        nc.scalar.activation(user_g[:, last, half:], user_planes[last][:].indirect(l_user[:, half // 16 :]), COPY)
+        nc.vector.tensor_copy(user_g[:, last, :half], user_planes[last].indirect(l_user[:, : half // 16]))
+        nc.scalar.activation(user_g[:, last, half:], user_planes[last].indirect(l_user[:, half // 16 :]), COPY)
 
         user_w = [held.tile([P, half, PACK], BF16, name=f"user_w{h}", align_bytes=64) for h in range(2)]
         user_c = [held.tile([P, half], U32, name=f"user_c{h}", align_bytes=64) for h in range(2)]
@@ -180,34 +184,64 @@ def tile_attend_tab_twosum_bestruns_kernel(
                 quantise_g(b - 1)
 
         ntile = E // P
-        for k in range(ntile):
+        turned, val_w, val_c, val_s = {}, {}, {}, {}
+
+        def gather_values(k, bank):
             val_g = held.tile([P, I], BF16, name=f"val_g{k}", align_bytes=64)
             if k < ntile - 1:
                 nc.scalar.activation(val_g[:], val_tiles[k][:].indirect(l_key[:]), COPY)
             else:
                 nc.vector.tensor_copy(val_g[:, : I // 2], val_tiles[k][:].indirect(l_key[:, : I // 32]))
                 nc.scalar.activation(val_g[:, I // 2 :], val_tiles[k][:].indirect(l_key[:, I // 32 :]), COPY)
+            return val_g
+
+        def turn_values(k, val_g, bank):
             words = val_g[:].bitcast(F32)
-            turned = psum_t.tile([P, 2, P], F32, name="turned")
+            turned[k] = psum_v.tile([P, 2, P], F32, name=f"turned{k}", tag=f"bank{bank}")
             for u in range(2):
-                nc.tensor.transpose(turned[:, u, :], words[:, u : I // 2 : 2], ident[:])
-            val_w = held.tile([P, P, PACK], BF16, name=f"val_w{k}", align_bytes=64)
-            nc.scalar.copy(out=val_w[:].bitcast(F32), in_=turned[:].rearrange("p u e -> p e u"))
-            val_c = held.tile([P, P], U32, name=f"val_c{k}", align_bytes=64)
-            val_s = held.tile([P, P], U8, name=f"val_s{k}", align_bytes=64)
-            nc.vector.quantize_mx(out=val_c[:].bitcast(FP8X4), scales=val_s[:], in_=val_w[:].rearrange("p e t -> p (e t)"))
-            o_bank = psum_o.tile([P, J], F32, name="o_bank")
+                nc.tensor.transpose(turned[k][:, u, :], words[:, u : I // 2 : 2], ident[:])
+
+        def weave_values(k, tag):
+            val_w[k] = held.tile([P, P, PACK], BF16, name=f"val_w{k}", tag=tag, align_bytes=64)
+            nc.scalar.copy(out=val_w[k][:].bitcast(F32), in_=turned[k][:].rearrange("p u e -> p e u"))
+
+        def quantise_values(k, tag):
+            val_c[k] = held.tile([P, P], U32, name=f"val_c{k}", tag=tag, align_bytes=64)
+            val_s[k] = held.tile([P, P], U8, name=f"val_s{k}", align_bytes=64)
+            nc.vector.quantize_mx(
+                out=val_c[k][:].bitcast(FP8X4), scales=val_s[k][:], in_=val_w[k][:].rearrange("p e t -> p (e t)")
+            )
+
+        def finish(k, bank, tag):
+            o_bank = psum_v.tile([P, J], F32, name=f"o_bank{k}", tag=f"bank{bank}")
             nc.tensor.matmul_mx(
                 out=o_bank[:],
-                lhsT=val_c[:].bitcast(FP8X4),
-                lhsT_scale=val_s[:],
+                lhsT=val_c[k][:].bitcast(FP8X4),
+                lhsT_scale=val_s[k][:],
                 rhs=g_c[:].bitcast(FP8X4),
                 rhs_scale=g_s[:],
                 start=True,
                 stop=True,
             )
-            best = held.tile([P, N], F32, name=f"best{k}", align_bytes=64)
+            best = held.tile([P, N], F32, name=f"best{k}", tag=tag, align_bytes=64)
             nc.vector.tensor_reduce(
                 best[:], o_bank[:].rearrange("p (n c) -> p n c", c=RUN), mybir.AxisListType.X, mybir.AluOpType.max
             )
             nc.sync.dma_start(out=out[k * P : (k + 1) * P, :], in_=best[:])
+
+        turn_values(0, gather_values(0, 0), 0)
+        turn_values(1, gather_values(1, 1), 1)
+        weave_values(0, "val1")
+        weave_values(1, "val_w1")
+        quantise_values(0, "val_c0")
+        quantise_values(1, "val_c1")
+        finish(0, 1, "best0")
+        finish(1, 0, "best1")
+        turn_values(2, gather_values(2, 2), 2)
+        turn_values(3, gather_values(3, 3), 3)
+        weave_values(2, "val3")
+        weave_values(3, "val_w3")
+        quantise_values(2, "val_c2")
+        quantise_values(3, "val_c3")
+        finish(2, 2, "val_w3")
+        finish(3, 3, "best3")

@@ -49,12 +49,16 @@ def tile_attend_tab_twosum_bestruns_kernel(
         rf = held.tile([P, PACK], F32, name="rf", align_bytes=64)
         ident = held.tile([P, P], F32, name="ident", align_bytes=64)
 
+        def load_scale_rows(dst, src, row0, r):
+            nc.gpsimd.dma_start(out=dst[row0 + r : P : 32, :].bitcast(I32), in_=src[0, r:16:4, :].bitcast(I32))
+
         nc.vector.memset(ks[:].bitcast(I32), 0)
         nc.vector.memset(ms[:].bitcast(I32), 0)
+        for r in range(4):
+            load_scale_rows(ks, keys_scales, 0, r)
+        for r in range(4):
+            load_scale_rows(ms, more_scales, MORE_ROW, r)
         make_identity(nc, ident[:])
-
-        def load_scale_rows(dst, src, row0, r):
-            nc.sync.dma_start(out=dst[row0 + r : P : 32, :].bitcast(I32), in_=src[0, r:16:4, :].bitcast(I32))
 
         notes_v = notes.rearrange("(p t) u -> p t u", t=PACK)
         users_v = users2.rearrange("(p t) u -> p t u", t=PACK)
@@ -62,14 +66,10 @@ def tile_attend_tab_twosum_bestruns_kernel(
         nc.sync.dma_start(l_note[:], offs2)
         nc.sync.dma_start(l_key[:], offs)
         nc.sync.dma_start(out=kw[:].bitcast(I32), in_=keys_words[0].rearrange("p n t -> p (n t)").bitcast(I32))
-        for r in range(4):
-            load_scale_rows(ks, keys_scales, 0, r)
         nc.sync.dma_start(out=note_pairs[1][:], in_=notes_v[:, 2:4, :])
         nc.sync.dma_start(l_user[:], offs4)
         nc.sync.dma_start(l_more[:], offs3)
         nc.sync.dma_start(out=user_pair[:], in_=users_v[:, 0:2, :])
-        for r in range(4):
-            load_scale_rows(ms, more_scales, MORE_ROW, r)
         nc.sync.dma_start(out=mw[:].bitcast(I32), in_=more_words[0].rearrange("p n t -> p (n t)").bitcast(I32))
         nc.sync.dma_start(out=user_late[0][:], in_=users_v[:, 2, :])
         nc.sync.dma_start(out=rf[:], in_=rowf.rearrange("(p t) o -> p (t o)", t=PACK))
@@ -201,9 +201,9 @@ def tile_attend_tab_twosum_bestruns_kernel(
             for u in range(2):
                 nc.tensor.transpose(turned[k][:, u, :], words[:, u : I // 2 : 2], ident[:])
 
-        def weave_values(k, tag):
+        def weave_values(k, tag, engine_copy):
             val_w[k] = held.tile([P, P, PACK], BF16, name=f"val_w{k}", tag=tag, align_bytes=64)
-            nc.scalar.copy(out=val_w[k][:].bitcast(F32), in_=turned[k][:].rearrange("p u e -> p e u"))
+            engine_copy(out=val_w[k][:].bitcast(F32), in_=turned[k][:].rearrange("p u e -> p e u"))
 
         def quantise_values(k, tag):
             val_c[k] = held.tile([P, P], U32, name=f"val_c{k}", tag=tag, align_bytes=64)
@@ -212,36 +212,42 @@ def tile_attend_tab_twosum_bestruns_kernel(
                 out=val_c[k][:].bitcast(FP8X4), scales=val_s[k][:], in_=val_w[k][:].rearrange("p e t -> p (e t)")
             )
 
-        def finish(k, bank, tag):
-            o_bank = psum_v.tile([P, J], F32, name=f"o_bank{k}", tag=f"bank{bank}")
-            nc.tensor.matmul_mx(
-                out=o_bank[:],
-                lhsT=val_c[k][:].bitcast(FP8X4),
-                lhsT_scale=val_s[k][:],
-                rhs=g_c[:].bitcast(FP8X4),
-                rhs_scale=g_s[:],
-                start=True,
-                stop=True,
-            )
+        def finish(k, banks, tag):
+            width = J // len(banks)
             best = held.tile([P, N], F32, name=f"best{k}", tag=tag, align_bytes=64)
-            nc.vector.tensor_reduce(
-                best[:], o_bank[:].rearrange("p (n c) -> p n c", c=RUN), mybir.AxisListType.X, mybir.AluOpType.max
-            )
+            for h, bank in enumerate(banks):
+                cols = slice(h * width, (h + 1) * width)
+                o_bank = psum_v.tile([P, width], F32, name=f"o_bank{k}_{h}", tag=f"bank{bank}")
+                nc.tensor.matmul_mx(
+                    out=o_bank[:],
+                    lhsT=val_c[k][:].bitcast(FP8X4),
+                    lhsT_scale=val_s[k][:],
+                    rhs=g_c[:, cols].bitcast(FP8X4),
+                    rhs_scale=g_s[:, cols],
+                    start=True,
+                    stop=True,
+                )
+                nc.vector.tensor_reduce(
+                    best[:, h * width // RUN : (h + 1) * width // RUN],
+                    o_bank[:].rearrange("p (n c) -> p n c", c=RUN),
+                    mybir.AxisListType.X,
+                    mybir.AluOpType.max,
+                )
             nc.sync.dma_start(out=out[k * P : (k + 1) * P, :], in_=best[:])
 
         turn_values(0, gather_values(0, 0), 0)
         turn_values(1, gather_values(1, 1), 1)
-        weave_values(0, "val1")
-        weave_values(1, "val_w1")
+        weave_values(0, "val1", nc.scalar.copy)
+        weave_values(1, "val_w1", nc.scalar.copy)
         quantise_values(0, "val_c0")
         quantise_values(1, "val_c1")
-        finish(0, 1, "best0")
-        finish(1, 0, "best1")
+        finish(0, [1], "best0")
+        finish(1, [0], "best1")
         turn_values(2, gather_values(2, 2), 2)
         turn_values(3, gather_values(3, 3), 3)
-        weave_values(2, "val3")
-        weave_values(3, "val_w3")
+        weave_values(2, "val3", nc.vector.tensor_copy)
+        weave_values(3, "val_w3", nc.scalar.copy)
         quantise_values(2, "val_c2")
         quantise_values(3, "val_c3")
-        finish(2, 2, "val_w3")
-        finish(3, 3, "best3")
+        finish(2, [2], "val_w3")
+        finish(3, [0, 1], "best3")

@@ -17,8 +17,11 @@ COPY = mybir.ActivationFunctionType.Copy
 
 P = 128
 PACK = 4
+PER_COLUMN = 16
+QUADRANT = 32
 RUN = J // N
-MORE_ROW = 4
+ALIGN = 64
+MORE_FIRST = 4
 
 
 def tile_attend_tab_twosum_bestruns_kernel(
@@ -31,70 +34,69 @@ def tile_attend_tab_twosum_bestruns_kernel(
         psum_g = ctx.enter_context(tc.psum_pool(name="psum_g", bufs=1))
         psum_v = ctx.enter_context(tc.psum_pool(name="psum_v", bufs=1))
 
-        l_key = lists.tile([P, I // 16], U16, name="l_key")
-        l_note = lists.tile([P, J // 16], U16, name="l_note")
-        l_more = lists.tile([P, I // 16], U16, name="l_more")
-        l_user = lists.tile([P, J // 16], U16, name="l_user")
+        l_key = lists.tile([P, I // PER_COLUMN], U16, name="l_key")
+        l_note = lists.tile([P, J // PER_COLUMN], U16, name="l_note")
+        l_more = lists.tile([P, I // PER_COLUMN], U16, name="l_more")
+        l_user = lists.tile([P, J // PER_COLUMN], U16, name="l_user")
 
-        kw = held.tile([P, T], U32, name="kw", align_bytes=64)
-        ks = held.tile([P, T], U8, name="ks", align_bytes=64)
-        mw = held.tile([P, X], U32, name="mw", align_bytes=64)
-        ms = held.tile([P, X], U8, name="ms", align_bytes=64)
-        note_pairs = [held.tile([P, 2, U], F32, name=f"note{u}", align_bytes=64) for u in range(2)]
-        user_pair = held.tile([P, 2, Z], F32, name="user_pair", align_bytes=64)
-        user_late = [held.tile([P, Z], F32, name=f"user_late{t}", align_bytes=64) for t in range(2)]
+        kw = held.tile([P, T], U32, name="kw", align_bytes=ALIGN)
+        ks = held.tile([P, T], U8, name="ks", align_bytes=ALIGN)
+        mw = held.tile([P, X], U32, name="mw", align_bytes=ALIGN)
+        ms = held.tile([P, X], U8, name="ms", align_bytes=ALIGN)
+        note_pairs = [held.tile([P, 2, U], F32, name=f"note{u}", align_bytes=ALIGN) for u in range(2)]
+        user_pair = held.tile([P, 2, Z], F32, name="user_pair", align_bytes=ALIGN)
+        user_late = [held.tile([P, Z], F32, name=f"user_late{t}", align_bytes=ALIGN) for t in range(2)]
         note_planes = [note_pairs[t // 2][:, t % 2, :] for t in range(PACK)]
         user_planes = [user_pair[:, 0, :], user_pair[:, 1, :], user_late[0][:], user_late[1][:]]
-        val_tiles = [held.tile([P, T], F32, name=f"val{k}", tag=f"val{k}", align_bytes=64) for k in range(E // P)]
-        rf = held.tile([P, PACK], F32, name="rf", align_bytes=64)
-        ident = held.tile([P, P], F32, name="ident", align_bytes=64)
-
-        def load_scale_rows(dst, src, row0, r):
-            nc.gpsimd.dma_start(out=dst[row0 + r : P : 32, :].bitcast(I32), in_=src[0, r:16:4, :].bitcast(I32))
+        ntile = E // P
+        val_tiles = [held.tile([P, T], F32, name=f"val{k}", tag=f"val{k}", align_bytes=ALIGN) for k in range(ntile)]
+        rf = held.tile([P, PACK], F32, name="rf", align_bytes=ALIGN)
+        ident = held.tile([P, P], F32, name="ident", align_bytes=ALIGN)
 
         nc.vector.memset(ks[:].bitcast(I32), 0)
         nc.vector.memset(ms[:].bitcast(I32), 0)
-        for r in range(4):
-            load_scale_rows(ks, keys_scales, 0, r)
-        for r in range(4):
-            load_scale_rows(ms, more_scales, MORE_ROW, r)
         make_identity(nc, ident[:])
+
+        def load_scale_rows(dst, src, first):
+            for r in range(4):
+                nc.sync.dma_start(
+                    out=dst[first + r : P : QUADRANT, :].bitcast(I32), in_=src[0, r:16:4, :].bitcast(I32)
+                )
+
+        def words_of(packed):
+            return packed[0].rearrange("p n t -> p (n t)").bitcast(I32)
 
         notes_v = notes.rearrange("(p t) u -> p t u", t=PACK)
         users_v = users2.rearrange("(p t) u -> p t u", t=PACK)
         nc.sync.dma_start(out=note_pairs[0][:], in_=notes_v[:, 0:2, :])
         nc.sync.dma_start(l_note[:], offs2)
         nc.sync.dma_start(l_key[:], offs)
-        nc.sync.dma_start(out=kw[:].bitcast(I32), in_=keys_words[0].rearrange("p n t -> p (n t)").bitcast(I32))
+        nc.sync.dma_start(out=kw[:].bitcast(I32), in_=words_of(keys_words))
+        load_scale_rows(ks, keys_scales, 0)
         nc.sync.dma_start(out=note_pairs[1][:], in_=notes_v[:, 2:4, :])
         nc.sync.dma_start(l_user[:], offs4)
         nc.sync.dma_start(l_more[:], offs3)
         nc.sync.dma_start(out=user_pair[:], in_=users_v[:, 0:2, :])
-        nc.sync.dma_start(out=mw[:].bitcast(I32), in_=more_words[0].rearrange("p n t -> p (n t)").bitcast(I32))
+        load_scale_rows(ms, more_scales, MORE_FIRST)
+        nc.sync.dma_start(out=mw[:].bitcast(I32), in_=words_of(more_words))
         nc.sync.dma_start(out=user_late[0][:], in_=users_v[:, 2, :])
         nc.sync.dma_start(out=rf[:], in_=rowf.rearrange("(p t) o -> p (t o)", t=PACK))
         nc.sync.dma_start(out=user_late[1][:], in_=users_v[:, 3, :])
-        for k in range(E // P):
+        for k in range(ntile):
             nc.sync.dma_start(out=val_tiles[k][:], in_=vals[k * P : (k + 1) * P, :])
 
-        kw_g = held.tile([P, I], U32, name="kw_g", align_bytes=64)
-        ks_g = held.tile([P, I], U8, name="ks_g", align_bytes=64)
-        mw_g = held.tile([P, I], U32, name="mw_g", align_bytes=64)
-        ms_g = held.tile([P, I], U8, name="ms_g", align_bytes=64)
+        kw_g = held.tile([P, I], U32, name="kw_g", align_bytes=ALIGN)
+        ks_g = held.tile([P, I], U8, name="ks_g", align_bytes=ALIGN)
+        mw_g = held.tile([P, I], U32, name="mw_g", align_bytes=ALIGN)
+        ms_g = held.tile([P, I], U8, name="ms_g", align_bytes=ALIGN)
 
         def dealt_gather(dst, window, offsets):
             nc.vector.tensor_copy(dst[:].rearrange("p (r s) -> p s r", r=PACK), window[:].indirect(offsets[:]))
 
-        dealt_gather(kw_g, kw, l_key)
-
-        note_g = held.tile([P, PACK, J], F32, name="note_g", align_bytes=64)
-        for t in range(PACK):
-            if t == 3:
-                dealt_gather(ks_g, ks, l_key)
-            if t % 2 == 0:
-                nc.scalar.activation(note_g[:, t, :], note_planes[t].indirect(l_note[:]), COPY)
-            else:
-                nc.vector.tensor_copy(note_g[:, t, :], note_planes[t].indirect(l_note[:]))
+        def shared_gather(dst, window, offsets):
+            slots, columns = dst.shape[1] // 2, offsets.shape[1] // 2
+            nc.vector.tensor_copy(dst[:, :slots], window.indirect(offsets[:, :columns]))
+            nc.scalar.activation(dst[:, slots:], window.indirect(offsets[:, columns:]), COPY)
 
         def weave(engine_copy, dst, src):
             engine_copy(
@@ -102,119 +104,104 @@ def tile_attend_tab_twosum_bestruns_kernel(
                 in_=src.rearrange("p t (c i) -> p c t i", i=4),
             )
 
-        note_w = held.tile([P, J, PACK], BF16, name="note_w", align_bytes=64)
-        note_c = held.tile([P, J], U32, name="note_c", align_bytes=64)
-        note_s = held.tile([P, J], U8, name="note_s", align_bytes=64)
+        def quantise(codes, scales, woven):
+            nc.vector.quantize_mx(out=codes.bitcast(FP8X4), scales=scales, in_=woven.rearrange("p c t -> p (c t)"))
+
+        dealt_gather(kw_g, kw, l_key)
+        note_g = held.tile([P, PACK, J], F32, name="note_g", align_bytes=ALIGN)
+        nc.scalar.activation(note_g[:, 0, :], note_planes[0].indirect(l_note[:]), COPY)
+        nc.vector.tensor_copy(note_g[:, 1, :], note_planes[1].indirect(l_note[:]))
+        nc.scalar.activation(note_g[:, 2, :], note_planes[2].indirect(l_note[:]), COPY)
+        dealt_gather(ks_g, ks, l_key)
+        nc.vector.tensor_copy(note_g[:, 3, :], note_planes[3].indirect(l_note[:]))
+
+        note_w = held.tile([P, J, PACK], BF16, name="note_w", align_bytes=ALIGN)
+        note_c = held.tile([P, J], U32, name="note_c", align_bytes=ALIGN)
+        note_s = held.tile([P, J], U8, name="note_s", align_bytes=ALIGN)
         weave(nc.vector.tensor_copy, note_w[:], note_g[:])
-        nc.vector.quantize_mx(out=note_c[:].bitcast(FP8X4), scales=note_s[:], in_=note_w[:].rearrange("p j t -> p (j t)"))
+        quantise(note_c[:], note_s[:], note_w[:])
 
         dealt_gather(ms_g, ms, l_more)
         dealt_gather(mw_g, mw, l_more)
 
         nblk = J // P
         g_banks = [psum_g.tile([P, PACK, P], F32, name=f"g{b}") for b in range(nblk)]
-        for b in range(nblk):
-            cols = slice(b * P, (b + 1) * P)
+
+        def table_passes(b, words, scales, first, codes, code_scales, opens):
             for r in range(PACK):
                 rows = slice(r * P, (r + 1) * P)
                 nc.tensor.matmul_mx(
                     out=g_banks[b][:, r, :],
-                    lhsT=kw_g[:, rows].bitcast(FP8X4),
-                    lhsT_scale=ks_g[:, rows],
-                    rhs=note_c[:, cols].bitcast(FP8X4),
-                    rhs_scale=note_s[:, cols],
-                    start=(r == 0),
-                    stop=False,
+                    lhsT=words[:, rows].bitcast(FP8X4),
+                    lhsT_scale=scales[first:, rows],
+                    rhs=codes.bitcast(FP8X4),
+                    rhs_scale=code_scales,
+                    start=(opens and r == 0),
+                    stop=(not opens and r == PACK - 1),
                 )
 
+        for b in range(nblk):
+            cols = slice(b * P, (b + 1) * P)
+            table_passes(b, kw_g, ks_g, 0, note_c[:, cols], note_s[:, cols], opens=True)
+
         half = J // 2
-        user_g = held.tile([P, PACK, J], F32, name="user_g", align_bytes=64)
+        user_g = held.tile([P, PACK, J], F32, name="user_g", align_bytes=ALIGN)
         for t in range(PACK - 1):
             nc.scalar.activation(user_g[:, t, :], user_planes[t].indirect(l_user[:]), COPY)
-        last = PACK - 1
-        nc.vector.tensor_copy(user_g[:, last, :half], user_planes[last].indirect(l_user[:, : half // 16]))
-        nc.scalar.activation(user_g[:, last, half:], user_planes[last].indirect(l_user[:, half // 16 :]), COPY)
+        shared_gather(user_g[:, PACK - 1, :], user_planes[PACK - 1], l_user)
 
-        user_w = [held.tile([P, half, PACK], BF16, name=f"user_w{h}", align_bytes=64) for h in range(2)]
-        user_c = [held.tile([P, half], U32, name=f"user_c{h}", align_bytes=64) for h in range(2)]
-        user_s = [held.tile([P, half], U8, name=f"user_s{h}", align_bytes=64) for h in range(2)]
+        user_w = [held.tile([P, half, PACK], BF16, name=f"user_w{h}", align_bytes=ALIGN) for h in range(2)]
+        user_c = [held.tile([P, half], U32, name=f"user_c{h}", align_bytes=ALIGN) for h in range(2)]
+        user_s = [held.tile([P, half], U8, name=f"user_s{h}", align_bytes=ALIGN) for h in range(2)]
         weave(nc.vector.tensor_copy, user_w[0][:], user_g[:, :, :half])
         weave(nc.scalar.copy, user_w[1][:], user_g[:, :, half:])
         for h in range(2):
-            nc.vector.quantize_mx(
-                out=user_c[h][:].bitcast(FP8X4), scales=user_s[h][:], in_=user_w[h][:].rearrange("p j t -> p (j t)")
-            )
+            quantise(user_c[h][:], user_s[h][:], user_w[h][:])
         for b in range(nblk):
             h, c0 = divmod(b * P, half)
             cols = slice(c0, c0 + P)
-            for r in range(PACK):
-                rows = slice(r * P, (r + 1) * P)
-                nc.tensor.matmul_mx(
-                    out=g_banks[b][:, r, :],
-                    lhsT=mw_g[:, rows].bitcast(FP8X4),
-                    lhsT_scale=ms_g[MORE_ROW:, rows],
-                    rhs=user_c[h][:, cols].bitcast(FP8X4),
-                    rhs_scale=user_s[h][:, cols],
-                    start=False,
-                    stop=(r == PACK - 1),
-                )
+            table_passes(b, mw_g, ms_g, MORE_FIRST, user_c[h][:, cols], user_s[h][:, cols], opens=False)
 
-        g_w = [held.tile([P, P, PACK], BF16, name=f"g_w{b}", align_bytes=64) for b in range(nblk)]
-        g_c = held.tile([P, J], U32, name="g_c", align_bytes=64)
-        g_s = held.tile([P, J], U8, name="g_s", align_bytes=64)
-
-        def scale_rows(b):
-            nc.vector.tensor_tensor(
-                g_w[b][:],
-                g_banks[b][:].rearrange("p r j -> p j r"),
-                rf[:].unsqueeze(1).to_broadcast([P, P, PACK]),
-                mybir.AluOpType.mult,
-            )
-
-        def quantise_g(b):
-            cols = slice(b * P, (b + 1) * P)
-            nc.vector.quantize_mx(
-                out=g_c[:, cols].bitcast(FP8X4), scales=g_s[:, cols], in_=g_w[b][:].rearrange("p j t -> p (j t)")
-            )
-
+        g_w = [held.tile([P, P, PACK], BF16, name=f"g_w{b}", align_bytes=ALIGN) for b in range(nblk)]
+        g_c = held.tile([P, J], U32, name="g_c", align_bytes=ALIGN)
+        g_s = held.tile([P, J], U8, name="g_s", align_bytes=ALIGN)
         for b in range(nblk + 1):
             if b < nblk:
-                scale_rows(b)
+                nc.vector.tensor_tensor(
+                    g_w[b][:],
+                    g_banks[b][:].rearrange("p r j -> p j r"),
+                    rf[:].unsqueeze(1).to_broadcast([P, P, PACK]),
+                    mybir.AluOpType.mult,
+                )
             if b > 0:
-                quantise_g(b - 1)
+                cols = slice((b - 1) * P, b * P)
+                quantise(g_c[:, cols], g_s[:, cols], g_w[b - 1][:])
 
-        ntile = E // P
         turned, val_w, val_c, val_s = {}, {}, {}, {}
 
-        def gather_values(k, bank):
-            val_g = held.tile([P, I], BF16, name=f"val_g{k}", align_bytes=64)
+        def gather_and_turn(k):
+            val_g = held.tile([P, I], BF16, name=f"val_g{k}", align_bytes=ALIGN)
             if k < ntile - 1:
                 nc.scalar.activation(val_g[:], val_tiles[k][:].indirect(l_key[:]), COPY)
             else:
-                nc.vector.tensor_copy(val_g[:, : I // 2], val_tiles[k][:].indirect(l_key[:, : I // 32]))
-                nc.scalar.activation(val_g[:, I // 2 :], val_tiles[k][:].indirect(l_key[:, I // 32 :]), COPY)
-            return val_g
-
-        def turn_values(k, val_g, bank):
+                shared_gather(val_g[:], val_tiles[k][:], l_key)
             words = val_g[:].bitcast(F32)
-            turned[k] = psum_v.tile([P, 2, P], F32, name=f"turned{k}", tag=f"bank{bank}")
+            turned[k] = psum_v.tile([P, 2, P], F32, name=f"turned{k}", tag=f"bank{k}")
             for u in range(2):
                 nc.tensor.transpose(turned[k][:, u, :], words[:, u : I // 2 : 2], ident[:])
 
-        def weave_values(k, tag, engine_copy):
-            val_w[k] = held.tile([P, P, PACK], BF16, name=f"val_w{k}", tag=tag, align_bytes=64)
-            engine_copy(out=val_w[k][:].bitcast(F32), in_=turned[k][:].rearrange("p u e -> p e u"))
+        def weave_values(k, tag):
+            val_w[k] = held.tile([P, P, PACK], BF16, name=f"val_w{k}", tag=tag, align_bytes=ALIGN)
+            nc.scalar.copy(out=val_w[k][:].bitcast(F32), in_=turned[k][:].rearrange("p u e -> p e u"))
 
-        def quantise_values(k, tag):
-            val_c[k] = held.tile([P, P], U32, name=f"val_c{k}", tag=tag, align_bytes=64)
-            val_s[k] = held.tile([P, P], U8, name=f"val_s{k}", align_bytes=64)
-            nc.vector.quantize_mx(
-                out=val_c[k][:].bitcast(FP8X4), scales=val_s[k][:], in_=val_w[k][:].rearrange("p e t -> p (e t)")
-            )
+        def quantise_values(k):
+            val_c[k] = held.tile([P, P], U32, name=f"val_c{k}", tag=f"val_c{k}", align_bytes=ALIGN)
+            val_s[k] = held.tile([P, P], U8, name=f"val_s{k}", align_bytes=ALIGN)
+            quantise(val_c[k][:], val_s[k][:], val_w[k][:])
 
         def finish(k, banks, tag):
             width = J // len(banks)
-            best = held.tile([P, N], F32, name=f"best{k}", tag=tag, align_bytes=64)
+            best = held.tile([P, N], F32, name=f"best{k}", tag=tag, align_bytes=ALIGN)
             for h, bank in enumerate(banks):
                 cols = slice(h * width, (h + 1) * width)
                 o_bank = psum_v.tile([P, width], F32, name=f"o_bank{k}_{h}", tag=f"bank{bank}")
@@ -235,19 +222,19 @@ def tile_attend_tab_twosum_bestruns_kernel(
                 )
             nc.sync.dma_start(out=out[k * P : (k + 1) * P, :], in_=best[:])
 
-        turn_values(0, gather_values(0, 0), 0)
-        turn_values(1, gather_values(1, 1), 1)
-        weave_values(0, "val1", nc.scalar.copy)
-        weave_values(1, "val_w1", nc.scalar.copy)
-        quantise_values(0, "val_c0")
-        quantise_values(1, "val_c1")
+        gather_and_turn(0)
+        gather_and_turn(1)
+        weave_values(0, "val1")
+        weave_values(1, "val_w1")
+        quantise_values(0)
+        quantise_values(1)
         finish(0, [1], "best0")
         finish(1, [0], "best1")
-        turn_values(2, gather_values(2, 2), 2)
-        turn_values(3, gather_values(3, 3), 3)
-        weave_values(2, "val3", nc.vector.tensor_copy)
-        weave_values(3, "val_w3", nc.scalar.copy)
-        quantise_values(2, "val_c2")
-        quantise_values(3, "val_c3")
+        gather_and_turn(2)
+        gather_and_turn(3)
+        weave_values(2, "val3")
+        weave_values(3, "val_w3")
+        quantise_values(2)
+        quantise_values(3)
         finish(2, [2], "val_w3")
         finish(3, [0, 1], "best3")

from contextlib import ExitStack

import concourse.mybir as mybir
from concourse.masks import make_identity

D, T, I, J, U, X, Z, E, N = 512, 2048, 512, 512, 1024, 1024, 1024, 512, 64
FLOPS = 2 * (2 * D * I * J + I * E * J)

F32 = mybir.dt.float32
BF16 = mybir.dt.bfloat16
I32 = mybir.dt.int32
U32 = mybir.dt.uint32
U16 = mybir.dt.uint16
U8 = mybir.dt.uint8
FP8X4 = mybir.dt.float8_e4m3fn_x4
COPY = mybir.ActivationFunctionType.Copy

P = 128
PACK = 4
PER_COLUMN = 16
QUADRANT = 32
RUN = J // N
ALIGN = 64
MORE_FIRST = 4


def tile_attend_tab_twosum_bestruns_kernel(
    tc, keys_words, keys_scales, notes, more_words, more_scales, users2, rowf, vals, offs, offs2, offs3, offs4, out
):
    nc = tc.nc
    with ExitStack() as ctx:
        lists = ctx.enter_context(tc.tile_pool(name="lists", bufs=1))
        held = ctx.enter_context(tc.tile_pool(name="held", bufs=1))
        psum_g = ctx.enter_context(tc.psum_pool(name="psum_g", bufs=1))
        psum_v = ctx.enter_context(tc.psum_pool(name="psum_v", bufs=1))

        l_key = lists.tile([P, I // PER_COLUMN], U16, name="l_key")
        l_note = lists.tile([P, J // PER_COLUMN], U16, name="l_note")
        l_more = lists.tile([P, I // PER_COLUMN], U16, name="l_more")
        l_user = lists.tile([P, J // PER_COLUMN], U16, name="l_user")

        kw = held.tile([P, T], U32, name="kw", align_bytes=ALIGN)
        ks = held.tile([P, T], U8, name="ks", align_bytes=ALIGN)
        mw = held.tile([P, X], U32, name="mw", align_bytes=ALIGN)
        ms = held.tile([P, X], U8, name="ms", align_bytes=ALIGN)
        note_pairs = [held.tile([P, 2, U], F32, name=f"note{u}", align_bytes=ALIGN) for u in range(2)]
        user_pair = held.tile([P, 2, Z], F32, name="user_pair", align_bytes=ALIGN)
        user_late = [held.tile([P, Z], F32, name=f"user_late{t}", align_bytes=ALIGN) for t in range(2)]
        note_planes = [note_pairs[t // 2][:, t % 2, :] for t in range(PACK)]
        user_planes = [user_pair[:, 0, :], user_pair[:, 1, :], user_late[0][:], user_late[1][:]]
        ntile = E // P
        val_tiles = [held.tile([P, T], F32, name=f"val{k}", tag=f"val{k}", align_bytes=ALIGN) for k in range(ntile)]
        rf = held.tile([P, PACK], F32, name="rf", align_bytes=ALIGN)
        ident = held.tile([P, P], F32, name="ident", align_bytes=ALIGN)

        nc.vector.memset(ks[:].bitcast(I32), 0)
        nc.vector.memset(ms[:].bitcast(I32), 0)
        make_identity(nc, ident[:])

        def load_scale_rows(dst, src, first):
            for r in range(4):
                nc.sync.dma_start(
                    out=dst[first + r : P : QUADRANT, :].bitcast(I32), in_=src[0, r:16:4, :].bitcast(I32)
                )

        def words_of(packed):
            return packed[0].rearrange("p n t -> p (n t)").bitcast(I32)

        notes_v = notes.rearrange("(p t) u -> p t u", t=PACK)
        users_v = users2.rearrange("(p t) u -> p t u", t=PACK)
        nc.sync.dma_start(out=note_pairs[0][:], in_=notes_v[:, 0:2, :])
        nc.sync.dma_start(l_note[:], offs2)
        nc.sync.dma_start(l_key[:], offs)
        nc.sync.dma_start(out=kw[:].bitcast(I32), in_=words_of(keys_words))
        load_scale_rows(ks, keys_scales, 0)
        nc.sync.dma_start(out=note_pairs[1][:], in_=notes_v[:, 2:4, :])
        nc.sync.dma_start(l_user[:], offs4)
        nc.sync.dma_start(l_more[:], offs3)
        nc.sync.dma_start(out=user_pair[:], in_=users_v[:, 0:2, :])
        load_scale_rows(ms, more_scales, MORE_FIRST)
        nc.sync.dma_start(out=mw[:].bitcast(I32), in_=words_of(more_words))
        nc.sync.dma_start(out=user_late[0][:], in_=users_v[:, 2, :])
        nc.sync.dma_start(out=rf[:], in_=rowf.rearrange("(p t) o -> p (t o)", t=PACK))
        nc.sync.dma_start(out=user_late[1][:], in_=users_v[:, 3, :])
        for k in range(ntile):
            nc.sync.dma_start(out=val_tiles[k][:], in_=vals[k * P : (k + 1) * P, :])

        kw_g = held.tile([P, I], U32, name="kw_g", align_bytes=ALIGN)
        ks_g = held.tile([P, I], U8, name="ks_g", align_bytes=ALIGN)
        mw_g = held.tile([P, I], U32, name="mw_g", align_bytes=ALIGN)
        ms_g = held.tile([P, I], U8, name="ms_g", align_bytes=ALIGN)

        def dealt_gather(dst, window, offsets):
            nc.vector.tensor_copy(dst[:].rearrange("p (r s) -> p s r", r=PACK), window[:].indirect(offsets[:]))

        def shared_gather(dst, window, offsets):
            slots, columns = dst.shape[1] // 2, offsets.shape[1] // 2
            nc.vector.tensor_copy(dst[:, :slots], window.indirect(offsets[:, :columns]))
            nc.scalar.activation(dst[:, slots:], window.indirect(offsets[:, columns:]), COPY)

        def weave(engine_copy, dst, src):
            engine_copy(
                out=dst.rearrange("p (c i) t -> p c t i", i=4),
                in_=src.rearrange("p t (c i) -> p c t i", i=4),
            )

        def quantise(codes, scales, woven):
            nc.vector.quantize_mx(out=codes.bitcast(FP8X4), scales=scales, in_=woven.rearrange("p c t -> p (c t)"))

        dealt_gather(kw_g, kw, l_key)
        note_g = held.tile([P, PACK, J], F32, name="note_g", align_bytes=ALIGN)
        nc.scalar.activation(note_g[:, 0, :], note_planes[0].indirect(l_note[:]), COPY)
        nc.vector.tensor_copy(note_g[:, 1, :], note_planes[1].indirect(l_note[:]))
        nc.scalar.activation(note_g[:, 2, :], note_planes[2].indirect(l_note[:]), COPY)
        dealt_gather(ks_g, ks, l_key)
        nc.vector.tensor_copy(note_g[:, 3, :], note_planes[3].indirect(l_note[:]))

        note_w = held.tile([P, J, PACK], BF16, name="note_w", align_bytes=ALIGN)
        note_c = held.tile([P, J], U32, name="note_c", align_bytes=ALIGN)
        note_s = held.tile([P, J], U8, name="note_s", align_bytes=ALIGN)
        weave(nc.vector.tensor_copy, note_w[:], note_g[:])
        quantise(note_c[:], note_s[:], note_w[:])

        dealt_gather(ms_g, ms, l_more)
        dealt_gather(mw_g, mw, l_more)

        nblk = J // P
        g_banks = [psum_g.tile([P, PACK, P], F32, name=f"g{b}") for b in range(nblk)]

        def table_passes(b, words, scales, first, codes, code_scales, opens):
            for r in range(PACK):
                rows = slice(r * P, (r + 1) * P)
                nc.tensor.matmul_mx(
                    out=g_banks[b][:, r, :],
                    lhsT=words[:, rows].bitcast(FP8X4),
                    lhsT_scale=scales[first:, rows],
                    rhs=codes.bitcast(FP8X4),
                    rhs_scale=code_scales,
                    start=(opens and r == 0),
                    stop=(not opens and r == PACK - 1),
                )

        for b in range(nblk):
            cols = slice(b * P, (b + 1) * P)
            table_passes(b, kw_g, ks_g, 0, note_c[:, cols], note_s[:, cols], opens=True)

        half = J // 2
        user_g = held.tile([P, PACK, J], F32, name="user_g", align_bytes=ALIGN)
        for t in range(PACK - 1):
            nc.scalar.activation(user_g[:, t, :], user_planes[t].indirect(l_user[:]), COPY)
        shared_gather(user_g[:, PACK - 1, :], user_planes[PACK - 1], l_user)

        user_w = [held.tile([P, half, PACK], BF16, name=f"user_w{h}", align_bytes=ALIGN) for h in range(2)]
        user_c = [held.tile([P, half], U32, name=f"user_c{h}", align_bytes=ALIGN) for h in range(2)]
        user_s = [held.tile([P, half], U8, name=f"user_s{h}", align_bytes=ALIGN) for h in range(2)]
        weave(nc.vector.tensor_copy, user_w[0][:], user_g[:, :, :half])
        weave(nc.scalar.copy, user_w[1][:], user_g[:, :, half:])
        for h in range(2):
            quantise(user_c[h][:], user_s[h][:], user_w[h][:])
        for b in range(nblk):
            h, c0 = divmod(b * P, half)
            cols = slice(c0, c0 + P)
            table_passes(b, mw_g, ms_g, MORE_FIRST, user_c[h][:, cols], user_s[h][:, cols], opens=False)

        g_w = [held.tile([P, P, PACK], BF16, name=f"g_w{b}", align_bytes=ALIGN) for b in range(nblk)]
        g_c = held.tile([P, J], U32, name="g_c", align_bytes=ALIGN)
        g_s = held.tile([P, J], U8, name="g_s", align_bytes=ALIGN)
        for b in range(nblk + 1):
            if b < nblk:
                nc.vector.tensor_tensor(
                    g_w[b][:],
                    g_banks[b][:].rearrange("p r j -> p j r"),
                    rf[:].unsqueeze(1).to_broadcast([P, P, PACK]),
                    mybir.AluOpType.mult,
                )
            if b > 0:
                cols = slice((b - 1) * P, b * P)
                quantise(g_c[:, cols], g_s[:, cols], g_w[b - 1][:])

        turned, val_w, val_c, val_s = {}, {}, {}, {}

        def gather_and_turn(k):
            val_g = held.tile([P, I], BF16, name=f"val_g{k}", align_bytes=ALIGN)
            if k < ntile - 1:
                nc.scalar.activation(val_g[:], val_tiles[k][:].indirect(l_key[:]), COPY)
            else:
                shared_gather(val_g[:], val_tiles[k][:], l_key)
            words = val_g[:].bitcast(F32)
            turned[k] = psum_v.tile([P, 2, P], F32, name=f"turned{k}", tag=f"bank{k}")
            for u in range(2):
                nc.tensor.transpose(turned[k][:, u, :], words[:, u : I // 2 : 2], ident[:])

        def weave_values(k, tag):
            val_w[k] = held.tile([P, P, PACK], BF16, name=f"val_w{k}", tag=tag, align_bytes=ALIGN)
            nc.scalar.copy(out=val_w[k][:].bitcast(F32), in_=turned[k][:].rearrange("p u e -> p e u"))

        def quantise_values(k):
            val_c[k] = held.tile([P, P], U32, name=f"val_c{k}", tag=f"val_c{k}", align_bytes=ALIGN)
            val_s[k] = held.tile([P, P], U8, name=f"val_s{k}", align_bytes=ALIGN)
            quantise(val_c[k][:], val_s[k][:], val_w[k][:])

        def finish(k, banks, tag):
            width = J // len(banks)
            best = held.tile([P, N], F32, name=f"best{k}", tag=tag, align_bytes=ALIGN)
            for h, bank in enumerate(banks):
                cols = slice(h * width, (h + 1) * width)
                o_bank = psum_v.tile([P, width], F32, name=f"o_bank{k}_{h}", tag=f"bank{bank}")
                nc.tensor.matmul_mx(
                    out=o_bank[:],
                    lhsT=val_c[k][:].bitcast(FP8X4),
                    lhsT_scale=val_s[k][:],
                    rhs=g_c[:, cols].bitcast(FP8X4),
                    rhs_scale=g_s[:, cols],
                    start=True,
                    stop=True,
                )
                nc.vector.tensor_reduce(
                    best[:, h * width // RUN : (h + 1) * width // RUN],
                    o_bank[:].rearrange("p (n c) -> p n c", c=RUN),
                    mybir.AxisListType.X,
                    mybir.AluOpType.max,
                )
            nc.sync.dma_start(out=out[k * P : (k + 1) * P, :], in_=best[:])

        gather_and_turn(0)
        gather_and_turn(1)
        weave_values(0, "val1")
        weave_values(1, "val_w1")
        quantise_values(0)
        quantise_values(1)
        finish(0, [1], "best0")
        finish(1, [0], "best1")
        gather_and_turn(2)
        gather_and_turn(3)
        weave_values(2, "val3")
        weave_values(3, "val_w3")
        quantise_values(2)
        quantise_values(3)
        finish(2, [2], "val_w3")
        finish(3, [0, 1], "best3")
